import numpy as np
import ml_dtypes


def mxq(x, axis, fmt="e4m3"):
    dtype, down = {"e4m3": (ml_dtypes.float8_e4m3fn, 7), "e5m2": (ml_dtypes.float8_e5m2, 14)}[fmt]
    v = np.moveaxis(np.asarray(x, np.float32).astype(ml_dtypes.bfloat16).astype(np.float64), axis, -1)
    blocks = v.reshape(v.shape[:-1] + (-1, 32))
    amax = np.abs(blocks).max(-1, keepdims=True)
    byte = np.maximum(np.where(amax > 0, np.frexp(amax)[1] - 1 + 127, 0) - down, 1)
    scale = np.exp2(byte - 127.0)
    codes = (blocks / scale).astype(np.float32).astype(dtype).astype(np.float64)
    return np.moveaxis((codes * scale).reshape(v.shape), -1, axis)


WIDE = False


def mx_kscale(k):
    if not WIDE:
        return np.ones(k)
    levels = np.array([30, -30])
    if k % 512:
        return np.exp2(np.random.permutation(np.resize(levels, k // 32))).repeat(32)
    a = np.empty((k // 512, 16))
    for p in range(k // 512):
        a[p, :8] = np.random.permutation(np.resize(levels, 8))
        for g in range(8):
            far = levels[np.abs(levels - a[p, g]) >= 10]
            a[p, g + 8] = far[np.random.randint(len(far))]
    return np.exp2(a.ravel()).repeat(32)


def f64(x):
    return np.asarray(x).astype(np.float64)


def striped(idx):
    return np.tile(np.asarray(idx).reshape(-1, 16).T, (8, 1)).astype(np.uint16)


def unstriped(offs):
    return offs[:16].T.reshape(-1).astype(np.int64)


E2M1 = np.array([0.0, 0.5, 1.0, 1.5, 2.0, 3.0, 4.0, 6.0, -0.0, -0.5, -1.0, -1.5, -2.0, -3.0, -4.0, -6.0])


def pack_weight(w, fmt):
    k, n = w.shape
    w = f64(np.asarray(w, np.float32).astype(ml_dtypes.bfloat16)).reshape(k // 32, 32, n)
    amax = np.abs(w).max(1)
    if fmt in ("e4m3", "e5m2"):
        byte = np.frexp(amax)[1] - 1 + 127 - (7 if fmt == "e4m3" else 14)
    else:
        mant, ex = np.frexp(amax / 6.0)
        byte = np.where(mant > 0.5, ex, ex - 1) + 127
    byte = np.clip(np.where(amax > 0, byte, 1), 1, 254)
    scaled = (w * np.exp2(127.0 - byte)[:, None, :]).reshape(k, n).astype(np.float32)
    by_word = np.ascontiguousarray(scaled.reshape(k // 512, 128, 4, n).transpose(0, 1, 3, 2))
    if fmt in ("e4m3", "e5m2"):
        words = by_word.astype(ml_dtypes.float8_e4m3fn if fmt == "e4m3" else ml_dtypes.float8_e5m2).view(np.uint8)
    else:
        c = by_word.astype(ml_dtypes.float4_e2m1fn).view(np.uint8) & 0xF
        words = (c[..., 0::2] | (c[..., 1::2] << 4)).reshape(k // 512, 128, 2 * n)
    return np.ascontiguousarray(words), np.ascontiguousarray(byte.astype(np.uint8).reshape(k // 512, 16, n))


def unpack_weight(words, scales, fmt):
    g, _, n = scales.shape
    words = np.ascontiguousarray(words).reshape(g, 128, n, -1)
    if fmt in ("e4m3", "e5m2"):
        vals = words.view(ml_dtypes.float8_e4m3fn if fmt == "e4m3" else ml_dtypes.float8_e5m2).astype(np.float64)
    else:
        nib = np.empty((g, 128, n, 4), np.uint8)
        nib[..., 0::2] = words & 0xF
        nib[..., 1::2] = words >> 4
        vals = E2M1[nib]
    vals = vals * np.repeat(np.exp2(scales.astype(np.float64) - 127.0), 8, axis=1)[..., None]
    return vals.transpose(0, 1, 3, 2).reshape(g * 512, n)


K, T, Z, J, R, C, O, N = 512, 1024, 1024, 256, 512, 512, 256, 256


def setup_inputs():
    n = np.random.standard_normal
    idx = np.random.permutation(T)[:J]
    idx2 = np.random.permutation(Z)[:J]
    idx3 = np.random.permutation(C)[:J]
    idx4 = np.random.permutation(C)[:J]
    idx5 = np.random.permutation(C)[:O]
    idx6 = np.random.permutation(C)[:O]
    fk = mx_kscale(K)
    fr = mx_kscale(R)
    xtp = pack_weight(n((K, T)) / fk[:, None], "e4m3")
    xop = pack_weight(n((K, Z)) / fk[:, None], "e2m1")
    wp = pack_weight(n((K, R)) * 1 / np.sqrt(K) * fk[:, None] * fr, "e5m2")
    w2p = pack_weight(n((K, R)) * 1 / np.sqrt(K) * fk[:, None] * fr, "e5m2")
    wbp = pack_weight(n((R, N)) * 1 / np.sqrt(R) / fr[:, None], "e5m2")
    return {
        "xt_words": xtp[0],
        "xt_scales": xtp[1],
        "xo_words": xop[0],
        "xo_scales": xop[1],
        "w_words": wp[0],
        "w_scales": wp[1],
        "w2_words": w2p[0],
        "w2_scales": w2p[1],
        "wb_words": wbp[0],
        "wb_scales": wbp[1],
        "offs": striped(idx),
        "offs2": striped(idx2),
        "offs3": striped(idx3),
        "offs4": striped(idx4),
        "offs5": striped(idx5),
        "offs6": striped(idx6),
    }


def reference(xt_words, xt_scales, xo_words, xo_scales, w_words, w_scales, w2_words, w2_scales, wb_words, wb_scales, offs, offs2, offs3, offs4, offs5, offs6):
    idx = unstriped(offs)
    idx2 = unstriped(offs2)
    idx3 = unstriped(offs3)
    idx4 = unstriped(offs4)
    idx5 = unstriped(offs5)
    idx6 = unstriped(offs6)
    xtu = unpack_weight(xt_words, xt_scales, "e4m3")
    xou = unpack_weight(xo_words, xo_scales, "e2m1")
    wu = unpack_weight(w_words, w_scales, "e5m2")
    w2u = unpack_weight(w2_words, w2_scales, "e5m2")
    wbu = unpack_weight(wb_words, wb_scales, "e5m2")
    xtidxg = xtu[:, idx]
    xoidx2g = xou[:, idx2]
    a = wu.T @ xtidxg + w2u.T @ xoidx2g
    b = w2u.T @ xtidxg + wu.T @ xoidx2g
    pw = np.zeros((R, C))
    pw[:, idx3] = a
    pv = np.zeros((R, C))
    pv[:, idx4] = b
    hid = np.abs(pw[:, idx5] - pv[:, idx6])
    hidq = mxq(hid, 0, "e4m3")
    y = wbu.T @ hidq
    return y

@@ -1,0 +1,193 @@
+from contextlib import ExitStack
+
+import concourse.mybir as mybir
+
+K, T, Z, J, R, C, O, N = 512, 1024, 1024, 256, 512, 512, 256, 256
+FLOPS = 2 * (4 * K * R * J + R * N * O)
+
+P = 128
+PACK = 4
+HALF = O // 2
+
+F32 = mybir.dt.float32
+BF16 = mybir.dt.bfloat16
+I32 = mybir.dt.int32
+U32 = mybir.dt.uint32
+U16 = mybir.dt.uint16
+U8 = mybir.dt.uint8
+E4M3 = mybir.dt.float8_e4m3fn_x4
+E5M2 = mybir.dt.float8_e5m2_x4
+E2M1 = mybir.dt.float4_e2m1fn_x4
+ACT = mybir.ActivationFunctionType
+ALU = mybir.AluOpType
+
+
+def tile_list_crossed_twoboards_one_plain_kernel(
+    tc, xt_words, xt_scales, xo_words, xo_scales, w_words, w_scales, w2_words, w2_scales,
+    wb_words, wb_scales, offs, offs2, offs3, offs4, offs5, offs6, out,
+):
+    nc = tc.nc
+    with ExitStack() as ctx:
+        lists = ctx.enter_context(tc.tile_pool(name="lists", bufs=1))
+        sb = ctx.enter_context(tc.tile_pool(name="sb", bufs=1))
+        ps = ctx.enter_context(tc.psum_pool(name="ps", bufs=1))
+
+        def load_list(name, src):
+            tile = lists.tile([P, J // 16], U16, name=name)
+            nc.sync.dma_start(tile[:], src)
+            return tile
+
+        def new_plane(name, width):
+            plane = sb.tile([P, width], U8, name=name, align_bytes=64)
+            return plane
+
+        def load_plane(plane, src, quadrants=range(4)):
+            width = src.shape[2] // 4
+            for q in quadrants:
+                rows = src[0, 4 * q : 4 * q + 4, :].bitcast(I32)
+                nc.sync.dma_start(
+                    plane[32 * q : 32 * q + 32, :].bitcast(I32), rows.unsqueeze(0).to_broadcast([8, 4, width])
+                )
+
+        def load_words(name, src, width):
+            tile = sb.tile([P, width], U32, name=name, align_bytes=64)
+            nc.sync.dma_start(tile[:].bitcast(I32), src[0].rearrange("p n t -> p (n t)").bitcast(I32))
+            return tile
+
+        xt_plane = new_plane("xt_plane", T)
+        xo_plane = new_plane("xo_plane", Z)
+        w_plane = new_plane("w_plane", R)
+        w2_plane = new_plane("w2_plane", R)
+        wb_plane = new_plane("wb_plane", N)
+        pw, pv = [], []
+        for t in range(PACK):
+            for boards, name in ((pw, "pw"), (pv, "pv")):
+                board = sb.tile([P, C], F32, name=name + str(t))
+                nc.gpsimd.memset(board[:], 0.0)
+                boards.append(board)
+
+        idx = load_list("idx", offs)
+        load_plane(xt_plane, xt_scales)
+        xt_tab = load_words("xt_tab", xt_words, T)
+        w_raw = load_words("w_raw", w_words, R)
+        w2_raw = load_words("w2_raw", w2_words, R)
+        idx2 = load_list("idx2", offs2)
+        load_plane(w_plane, w_scales)
+        xo_tab = sb.tile([P, Z], U16, name="xo_tab", align_bytes=64)
+        nc.sync.dma_start(xo_tab[:].bitcast(I32), xo_words[0].bitcast(I32))
+        load_plane(w2_plane, w2_scales)
+        load_plane(xo_plane, xo_scales)
+        idx3 = load_list("idx3", offs3)
+        idx4 = load_list("idx4", offs4)
+        idx6 = load_list("idx6", offs6)
+        idx5 = load_list("idx5", offs5)
+        wb_codes = load_words("wb_codes", wb_words, N)
+        load_plane(wb_plane, wb_scales)
+
+        xt_codes = sb.tile([P, J], U32, name="xt_codes", align_bytes=64)
+        xt_sc = sb.tile([P, J], U8, name="xt_sc", align_bytes=64)
+        xo_codes = sb.tile([P, J], U16, name="xo_codes", align_bytes=64)
+        xo_sc = sb.tile([P, J], U8, name="xo_sc", align_bytes=64)
+        nc.vector.tensor_copy(xt_sc[:], xt_plane[:].indirect(idx[:]))
+        nc.vector.tensor_copy(xt_codes[:], xt_tab[:].indirect(idx[:]))
+
+        def deal(name, raw, plane):
+            codes = sb.tile([P, R], U32, name=name + "_codes", align_bytes=64)
+            scales = sb.tile([P, R], U8, name=name + "_sc", align_bytes=64)
+            nc.scalar.copy(
+                codes[:].rearrange("p (t m) -> p m t", t=PACK), raw[:].rearrange("p (m t) -> p m t", t=PACK)
+            )
+            nc.vector.tensor_copy(
+                scales[:].rearrange("p (t m) -> p t m", t=PACK), plane[:].rearrange("p (m t) -> p t m", t=PACK)
+            )
+            return codes, scales
+
+        w = deal("w", w_raw, w_plane)
+        nc.vector.tensor_copy(xo_codes[:], xo_tab[:].indirect(idx2[:]))
+        w2 = deal("w2", w2_raw, w2_plane)
+        nc.vector.tensor_copy(xo_sc[:], xo_plane[:].indirect(idx2[:]))
+
+        def first_stage(bank, t, weight, codes, scales, first):
+            cols = slice(t * P, (t + 1) * P)
+            nc.tensor.matmul_mx(
+                bank[:], lhsT=weight[0][:, cols].bitcast(E5M2), lhsT_scale=weight[1][:, cols],
+                rhs=codes, rhs_scale=scales, start=first, stop=not first,
+            )
+
+        a_bank = [ps.tile([P, J], F32, name="a_bank" + str(t)) for t in range(PACK)]
+        b_bank = [ps.tile([P, J], F32, name="b_bank" + str(t)) for t in range(PACK)]
+        for banks, weight in ((a_bank, w), (b_bank, w2)):
+            for t in range(PACK):
+                first_stage(banks[t], t, weight, xt_codes[:].bitcast(E4M3), xt_sc[:], True)
+        for t in range(PACK):
+            for banks, weight in ((a_bank, w2), (b_bank, w)):
+                first_stage(banks[t], t, weight, xo_codes[:].bitcast(E2M1), xo_sc[:], False)
+
+        a_sb = [sb.tile([P, J], F32, name="a_sb" + str(t)) for t in range(PACK)]
+        b_sb = [sb.tile([P, J], F32, name="b_sb" + str(t)) for t in range(PACK)]
+        pv_read = [[sb.tile([P, HALF], F32, name="pv_read%d_%d" % (t, h)) for h in range(2)] for t in range(PACK)]
+        diff = [sb.tile([P, PACK, HALF], F32, name="diff" + str(h)) for h in range(2)]
+
+        def half_of(lst, h):
+            return lst[:, h * (HALF // 16) : (h + 1) * (HALF // 16)]
+
+        def empty_a(t):
+            nc.vector.tensor_copy(a_sb[t][:], a_bank[t][:])
+
+        def empty_b(t):
+            nc.scalar.activation(b_sb[t][:], b_bank[t][:], ACT.Copy)
+
+        def put_a(t):
+            nc.vector.tensor_copy(pw[t][:].indirect(idx3[:]), a_sb[t][:])
+
+        def put_b(t):
+            nc.scalar.activation(pv[t][:].indirect(idx4[:]), b_sb[t][:], ACT.Copy)
+
+        def read_pv(t, h):
+            nc.scalar.activation(pv_read[t][h][:], pv[t][:].indirect(half_of(idx6, h)), ACT.Copy)
+
+        def read_diff(t, h):
+            nc.vector.tensor_tensor(
+                diff[h][:, t, :], pw[t][:].indirect(half_of(idx5, h)), pv_read[t][h][:], ALU.subtract
+            )
+
+        empty_a(0)
+        empty_b(0)
+        for t in range(PACK):
+            if t + 1 < PACK:
+                empty_a(t + 1)
+                empty_b(t + 1)
+            put_a(t)
+            put_b(t)
+            if t >= 1:
+                read_pv(t - 1, 0)
+                if t - 1 < 2:
+                    read_pv(t - 1, 1)
+        read_pv(3, 0)
+        read_pv(2, 1)
+        read_pv(3, 1)
+        for t, h in ((0, 0), (1, 0), (0, 1), (2, 0), (3, 0), (1, 1), (2, 1), (3, 1)):
+            read_diff(t, h)
+
+        for h in range(2):
+            hid = sb.tile([P, HALF, PACK], BF16, name="hid" + str(h), align_bytes=64)
+            nc.scalar.activation(
+                hid[:].rearrange("p (c i) t -> p c t i", i=4),
+                diff[h][:].rearrange("p t (c i) -> p c t i", i=4),
+                ACT.Abs,
+            )
+            hid_codes = sb.tile([P, HALF], U32, name="hid_codes" + str(h), align_bytes=64)
+            hid_sc = sb.tile([P, HALF], U8, name="hid_sc" + str(h), align_bytes=64)
+            nc.vector.quantize_mx(hid_codes[:].bitcast(E4M3), hid_sc[:], hid[:].rearrange("p o t -> p (o t)"))
+            y_bank = ps.tile([P, 2, HALF], F32, name="a_bank" + str(h))
+            for nb in range(2):
+                cols = slice(nb * P, (nb + 1) * P)
+                nc.tensor.matmul_mx(
+                    y_bank[:, nb, :], lhsT=wb_codes[:, cols].bitcast(E5M2), lhsT_scale=wb_plane[:, cols],
+                    rhs=hid_codes[:].bitcast(E4M3), rhs_scale=hid_sc[:], start=True, stop=True,
+                )
+            y_sb = sb.tile([P, 2, HALF], F32, name="y_sb" + str(h))
+            nc.vector.tensor_copy(y_sb[:], y_bank[:])
+            nc.sync.dma_start(
+                out[:, h * HALF : (h + 1) * HALF].rearrange("(b p) o -> p b o", p=P), y_sb[:]
+            )

@@ -38,14 +38,19 @@ def tile_list_crossed_twoboards_one_plain_kernel(
             return tile
 
         def new_plane(name, width):
-            plane = sb.tile([P, width], U8, name=name, align_bytes=64)
-            return plane
+            return sb.tile([P, width], U8, name=name, align_bytes=64)
 
-        def load_plane(plane, src, quadrants=range(4)):
+        def load_plane(plane, src, quadrants=range(4), queue=nc.sync):
+            for q in quadrants:
+                queue.dma_start(
+                    plane[32 * q : 32 * q + 4, :].bitcast(I32), src[0, 4 * q : 4 * q + 4, :].bitcast(I32)
+                )
+
+        def load_plane_whole(plane, src, quadrants=range(4), queue=nc.sync):
             width = src.shape[2] // 4
             for q in quadrants:
                 rows = src[0, 4 * q : 4 * q + 4, :].bitcast(I32)
-                nc.sync.dma_start(
+                queue.dma_start(
                     plane[32 * q : 32 * q + 32, :].bitcast(I32), rows.unsqueeze(0).to_broadcast([8, 4, width])
                 )
 
@@ -59,6 +64,9 @@ def tile_list_crossed_twoboards_one_plain_kernel(
         w_plane = new_plane("w_plane", R)
         w2_plane = new_plane("w2_plane", R)
         wb_plane = new_plane("wb_plane", N)
+        load_plane_whole(w_plane, w_scales, range(2), nc.gpsimd)
+        for plane in (xo_plane, w2_plane, wb_plane):
+            nc.vector.memset(plane[:].bitcast(I32), 0)
         pw, pv = [], []
         for t in range(PACK):
             for boards, name in ((pw, "pw"), (pv, "pv")):
@@ -67,16 +75,16 @@ def tile_list_crossed_twoboards_one_plain_kernel(
                 boards.append(board)
 
         idx = load_list("idx", offs)
-        load_plane(xt_plane, xt_scales)
+        load_plane_whole(xt_plane, xt_scales)
+        idx2 = load_list("idx2", offs2)
         xt_tab = load_words("xt_tab", xt_words, T)
         w_raw = load_words("w_raw", w_words, R)
-        w2_raw = load_words("w2_raw", w2_words, R)
-        idx2 = load_list("idx2", offs2)
-        load_plane(w_plane, w_scales)
+        load_plane_whole(w_plane, w_scales, range(2, 4))
+        load_plane(xo_plane, xo_scales)
         xo_tab = sb.tile([P, Z], U16, name="xo_tab", align_bytes=64)
         nc.sync.dma_start(xo_tab[:].bitcast(I32), xo_words[0].bitcast(I32))
+        w2_raw = load_words("w2_raw", w2_words, R)
         load_plane(w2_plane, w2_scales)
-        load_plane(xo_plane, xo_scales)
         idx3 = load_list("idx3", offs3)
         idx4 = load_list("idx4", offs4)
         idx6 = load_list("idx6", offs6)
@@ -91,21 +99,24 @@ def tile_list_crossed_twoboards_one_plain_kernel(
         nc.vector.tensor_copy(xt_sc[:], xt_plane[:].indirect(idx[:]))
         nc.vector.tensor_copy(xt_codes[:], xt_tab[:].indirect(idx[:]))
 
-        def deal(name, raw, plane):
+        def deal(name, raw, plane, runs):
             codes = sb.tile([P, R], U32, name=name + "_codes", align_bytes=64)
             scales = sb.tile([P, R], U8, name=name + "_sc", align_bytes=64)
-            nc.scalar.copy(
-                codes[:].rearrange("p (t m) -> p m t", t=PACK), raw[:].rearrange("p (m t) -> p m t", t=PACK)
-            )
-            nc.vector.tensor_copy(
-                scales[:].rearrange("p (t m) -> p t m", t=PACK), plane[:].rearrange("p (m t) -> p t m", t=PACK)
-            )
+            for run in runs:
+                nc.scalar.copy(
+                    codes[:].rearrange("p (t m) -> p m t", t=PACK)[:, :, run],
+                    raw[:].rearrange("p (m t) -> p m t", t=PACK)[:, :, run],
+                )
+                nc.vector.tensor_copy(
+                    scales[:].rearrange("p (t m) -> p t m", t=PACK)[:, run, :],
+                    plane[:].rearrange("p (m t) -> p t m", t=PACK)[:, run, :],
+                )
             return codes, scales
 
-        w = deal("w", w_raw, w_plane)
-        nc.vector.tensor_copy(xo_codes[:], xo_tab[:].indirect(idx2[:]))
-        w2 = deal("w2", w2_raw, w2_plane)
+        w = deal("w", w_raw, w_plane, [slice(0, PACK)])
         nc.vector.tensor_copy(xo_sc[:], xo_plane[:].indirect(idx2[:]))
+        nc.vector.tensor_copy(xo_codes[:], xo_tab[:].indirect(idx2[:]))
+        w2 = deal("w2", w2_raw, w2_plane, [slice(0, 1), slice(1, PACK)])
 
         def first_stage(bank, t, weight, codes, scales, first):
             cols = slice(t * P, (t + 1) * P)
@@ -116,12 +127,17 @@ def tile_list_crossed_twoboards_one_plain_kernel(
 
         a_bank = [ps.tile([P, J], F32, name="a_bank" + str(t)) for t in range(PACK)]
         b_bank = [ps.tile([P, J], F32, name="b_bank" + str(t)) for t in range(PACK)]
-        for banks, weight in ((a_bank, w), (b_bank, w2)):
-            for t in range(PACK):
-                first_stage(banks[t], t, weight, xt_codes[:].bitcast(E4M3), xt_sc[:], True)
+        xt_operand = (xt_codes[:].bitcast(E4M3), xt_sc[:])
+        xo_operand = (xo_codes[:].bitcast(E2M1), xo_sc[:])
         for t in range(PACK):
-            for banks, weight in ((a_bank, w2), (b_bank, w)):
-                first_stage(banks[t], t, weight, xo_codes[:].bitcast(E2M1), xo_sc[:], False)
+            first_stage(a_bank[t], t, w, *xt_operand, True)
+        first_stage(b_bank[0], 0, w, *xo_operand, True)
+        first_stage(a_bank[0], 0, w2, *xo_operand, False)
+        first_stage(b_bank[0], 0, w2, *xt_operand, False)
+        for t in range(1, PACK):
+            first_stage(a_bank[t], t, w2, *xo_operand, False)
+            first_stage(b_bank[t], t, w2, *xt_operand, True)
+            first_stage(b_bank[t], t, w, *xo_operand, False)
 
         a_sb = [sb.tile([P, J], F32, name="a_sb" + str(t)) for t in range(PACK)]
         b_sb = [sb.tile([P, J], F32, name="b_sb" + str(t)) for t in range(PACK)]
@@ -144,7 +160,10 @@ def tile_list_crossed_twoboards_one_plain_kernel(
             nc.scalar.activation(pv[t][:].indirect(idx4[:]), b_sb[t][:], ACT.Copy)
 
         def read_pv(t, h):
-            nc.scalar.activation(pv_read[t][h][:], pv[t][:].indirect(half_of(idx6, h)), ACT.Copy)
+            if (t, h) == (0, 0):
+                nc.vector.tensor_copy(pv_read[t][h][:], pv[t][:].indirect(half_of(idx6, h)))
+            else:
+                nc.scalar.activation(pv_read[t][h][:], pv[t][:].indirect(half_of(idx6, h)), ACT.Copy)
 
         def read_diff(t, h):
             nc.vector.tensor_tensor(
@@ -179,15 +198,18 @@ def tile_list_crossed_twoboards_one_plain_kernel(
             hid_codes = sb.tile([P, HALF], U32, name="hid_codes" + str(h), align_bytes=64)
             hid_sc = sb.tile([P, HALF], U8, name="hid_sc" + str(h), align_bytes=64)
             nc.vector.quantize_mx(hid_codes[:].bitcast(E4M3), hid_sc[:], hid[:].rearrange("p o t -> p (o t)"))
-            y_bank = ps.tile([P, 2, HALF], F32, name="a_bank" + str(h))
             for nb in range(2):
                 cols = slice(nb * P, (nb + 1) * P)
+                y_bank = ps.tile([P, HALF], F32, name=("a_bank", "b_bank")[nb] + str(h))
                 nc.tensor.matmul_mx(
-                    y_bank[:, nb, :], lhsT=wb_codes[:, cols].bitcast(E5M2), lhsT_scale=wb_plane[:, cols],
+                    y_bank[:], lhsT=wb_codes[:, cols].bitcast(E5M2), lhsT_scale=wb_plane[:, cols],
                     rhs=hid_codes[:].bitcast(E4M3), rhs_scale=hid_sc[:], start=True, stop=True,
                 )
-            y_sb = sb.tile([P, 2, HALF], F32, name="y_sb" + str(h))
-            nc.vector.tensor_copy(y_sb[:], y_bank[:])
-            nc.sync.dma_start(
-                out[:, h * HALF : (h + 1) * HALF].rearrange("(b p) o -> p b o", p=P), y_sb[:]
-            )
+                y_sb = sb.tile([P, HALF], F32, name="y_sb%d_%d" % (h, nb))
+                place = out[cols, h * HALF : (h + 1) * HALF]
+                if (h, nb) == (1, 1):
+                    nc.scalar.copy(y_sb[:], y_bank[:])
+                    nc.scalar.dma_start(place, y_sb[:])
+                else:
+                    nc.vector.tensor_copy(y_sb[:], y_bank[:])
+                    nc.sync.dma_start(place, y_sb[:])

@@ -64,26 +64,27 @@ def tile_list_crossed_twoboards_one_plain_kernel(
         w_plane = new_plane("w_plane", R)
         w2_plane = new_plane("w2_plane", R)
         wb_plane = new_plane("wb_plane", N)
-        load_plane_whole(w_plane, w_scales, range(2), nc.gpsimd)
-        for plane in (xo_plane, w2_plane, wb_plane):
-            nc.vector.memset(plane[:].bitcast(I32), 0)
+        nc.vector.memset(xo_plane[:].bitcast(I32), 0)
+        for plane in (xt_plane, w2_plane, wb_plane):
+            nc.gpsimd.memset(plane[:].bitcast(I32), 0)
         pw, pv = [], []
         for t in range(PACK):
             for boards, name in ((pw, "pw"), (pv, "pv")):
                 board = sb.tile([P, C], F32, name=name + str(t))
-                nc.gpsimd.memset(board[:], 0.0)
+                nc.vector.memset(board[:], 0.0)
                 boards.append(board)
 
         idx = load_list("idx", offs)
-        load_plane_whole(xt_plane, xt_scales)
+        load_plane_whole(w_plane, w_scales)
         idx2 = load_list("idx2", offs2)
         xt_tab = load_words("xt_tab", xt_words, T)
         w_raw = load_words("w_raw", w_words, R)
-        load_plane_whole(w_plane, w_scales, range(2, 4))
-        load_plane(xo_plane, xo_scales)
+        load_plane(xt_plane, xt_scales)
+        load_plane(xo_plane, xo_scales, range(2))
         xo_tab = sb.tile([P, Z], U16, name="xo_tab", align_bytes=64)
         nc.sync.dma_start(xo_tab[:].bitcast(I32), xo_words[0].bitcast(I32))
         w2_raw = load_words("w2_raw", w2_words, R)
+        load_plane(xo_plane, xo_scales, range(2, 4))
         load_plane(w2_plane, w2_scales)
         idx3 = load_list("idx3", offs3)
         idx4 = load_list("idx4", offs4)
@@ -96,8 +97,6 @@ def tile_list_crossed_twoboards_one_plain_kernel(
         xt_sc = sb.tile([P, J], U8, name="xt_sc", align_bytes=64)
         xo_codes = sb.tile([P, J], U16, name="xo_codes", align_bytes=64)
         xo_sc = sb.tile([P, J], U8, name="xo_sc", align_bytes=64)
-        nc.vector.tensor_copy(xt_sc[:], xt_plane[:].indirect(idx[:]))
-        nc.vector.tensor_copy(xt_codes[:], xt_tab[:].indirect(idx[:]))
 
         def deal(name, raw, plane, runs):
             codes = sb.tile([P, R], U32, name=name + "_codes", align_bytes=64)
@@ -114,8 +113,10 @@ def tile_list_crossed_twoboards_one_plain_kernel(
             return codes, scales
 
         w = deal("w", w_raw, w_plane, [slice(0, PACK)])
-        nc.vector.tensor_copy(xo_sc[:], xo_plane[:].indirect(idx2[:]))
+        nc.vector.tensor_copy(xt_codes[:], xt_tab[:].indirect(idx[:]))
+        nc.vector.tensor_copy(xt_sc[:], xt_plane[:].indirect(idx[:]))
         nc.vector.tensor_copy(xo_codes[:], xo_tab[:].indirect(idx2[:]))
+        nc.vector.tensor_copy(xo_sc[:], xo_plane[:].indirect(idx2[:]))
         w2 = deal("w2", w2_raw, w2_plane, [slice(0, 1), slice(1, PACK)])
 
         def first_stage(bank, t, weight, codes, scales, first):

@@ -71,7 +71,7 @@ def tile_list_crossed_twoboards_one_plain_kernel(
         for t in range(PACK):
             for boards, name in ((pw, "pw"), (pv, "pv")):
                 board = sb.tile([P, C], F32, name=name + str(t))
-                nc.vector.memset(board[:], 0.0)
+                (nc.vector if t < 2 else nc.gpsimd).memset(board[:], 0.0)
                 boards.append(board)
 
         idx = load_list("idx", offs)

from contextlib import ExitStack

import concourse.mybir as mybir

K, T, Z, J, R, C, O, N = 512, 1024, 1024, 256, 512, 512, 256, 256
FLOPS = 2 * (4 * K * R * J + R * N * O)

P = 128
PACK = 4
HALF = O // 2

F32 = mybir.dt.float32
BF16 = mybir.dt.bfloat16
I32 = mybir.dt.int32
U32 = mybir.dt.uint32
U16 = mybir.dt.uint16
U8 = mybir.dt.uint8
E4M3 = mybir.dt.float8_e4m3fn_x4
E5M2 = mybir.dt.float8_e5m2_x4
E2M1 = mybir.dt.float4_e2m1fn_x4
ACT = mybir.ActivationFunctionType
ALU = mybir.AluOpType


def tile_list_crossed_twoboards_one_plain_kernel(
    tc, xt_words, xt_scales, xo_words, xo_scales, w_words, w_scales, w2_words, w2_scales,
    wb_words, wb_scales, offs, offs2, offs3, offs4, offs5, offs6, out,
):
    nc = tc.nc
    with ExitStack() as ctx:
        lists = ctx.enter_context(tc.tile_pool(name="lists", bufs=1))
        sb = ctx.enter_context(tc.tile_pool(name="sb", bufs=1))
        ps = ctx.enter_context(tc.psum_pool(name="ps", bufs=1))

        def load_list(name, src):
            tile = lists.tile([P, J // 16], U16, name=name)
            nc.sync.dma_start(tile[:], src)
            return tile

        def new_plane(name, width):
            return sb.tile([P, width], U8, name=name, align_bytes=64)

        def load_plane(plane, src, quadrants=range(4), queue=nc.sync):
            for q in quadrants:
                queue.dma_start(
                    plane[32 * q : 32 * q + 4, :].bitcast(I32), src[0, 4 * q : 4 * q + 4, :].bitcast(I32)
                )

        def load_plane_whole(plane, src, quadrants=range(4), queue=nc.sync):
            width = src.shape[2] // 4
            for q in quadrants:
                rows = src[0, 4 * q : 4 * q + 4, :].bitcast(I32)
                queue.dma_start(
                    plane[32 * q : 32 * q + 32, :].bitcast(I32), rows.unsqueeze(0).to_broadcast([8, 4, width])
                )

        def load_words(name, src, width):
            tile = sb.tile([P, width], U32, name=name, align_bytes=64)
            nc.sync.dma_start(tile[:].bitcast(I32), src[0].rearrange("p n t -> p (n t)").bitcast(I32))
            return tile

        xt_plane = new_plane("xt_plane", T)
        xo_plane = new_plane("xo_plane", Z)
        w_plane = new_plane("w_plane", R)
        w2_plane = new_plane("w2_plane", R)
        wb_plane = new_plane("wb_plane", N)
        nc.vector.memset(xo_plane[:].bitcast(I32), 0)
        for plane in (xt_plane, w2_plane, wb_plane):
            nc.gpsimd.memset(plane[:].bitcast(I32), 0)
        pw, pv = [], []
        for t in range(PACK):
            for boards, name in ((pw, "pw"), (pv, "pv")):
                board = sb.tile([P, C], F32, name=name + str(t))
                (nc.vector if t < 2 else nc.gpsimd).memset(board[:], 0.0)
                boards.append(board)

        idx = load_list("idx", offs)
        load_plane_whole(w_plane, w_scales)
        idx2 = load_list("idx2", offs2)
        xt_tab = load_words("xt_tab", xt_words, T)
        w_raw = load_words("w_raw", w_words, R)
        load_plane(xt_plane, xt_scales)
        load_plane(xo_plane, xo_scales, range(2))
        xo_tab = sb.tile([P, Z], U16, name="xo_tab", align_bytes=64)
        nc.sync.dma_start(xo_tab[:].bitcast(I32), xo_words[0].bitcast(I32))
        w2_raw = load_words("w2_raw", w2_words, R)
        load_plane(xo_plane, xo_scales, range(2, 4))
        load_plane(w2_plane, w2_scales)
        idx3 = load_list("idx3", offs3)
        idx4 = load_list("idx4", offs4)
        idx6 = load_list("idx6", offs6)
        idx5 = load_list("idx5", offs5)
        wb_codes = load_words("wb_codes", wb_words, N)
        load_plane(wb_plane, wb_scales)

        xt_codes = sb.tile([P, J], U32, name="xt_codes", align_bytes=64)
        xt_sc = sb.tile([P, J], U8, name="xt_sc", align_bytes=64)
        xo_codes = sb.tile([P, J], U16, name="xo_codes", align_bytes=64)
        xo_sc = sb.tile([P, J], U8, name="xo_sc", align_bytes=64)

        def deal(name, raw, plane, runs):
            codes = sb.tile([P, R], U32, name=name + "_codes", align_bytes=64)
            scales = sb.tile([P, R], U8, name=name + "_sc", align_bytes=64)
            for run in runs:
                nc.scalar.copy(
                    codes[:].rearrange("p (t m) -> p m t", t=PACK)[:, :, run],
                    raw[:].rearrange("p (m t) -> p m t", t=PACK)[:, :, run],
                )
                nc.vector.tensor_copy(
                    scales[:].rearrange("p (t m) -> p t m", t=PACK)[:, run, :],
                    plane[:].rearrange("p (m t) -> p t m", t=PACK)[:, run, :],
                )
            return codes, scales

        w = deal("w", w_raw, w_plane, [slice(0, PACK)])
        nc.vector.tensor_copy(xt_codes[:], xt_tab[:].indirect(idx[:]))
        nc.vector.tensor_copy(xt_sc[:], xt_plane[:].indirect(idx[:]))
        nc.vector.tensor_copy(xo_codes[:], xo_tab[:].indirect(idx2[:]))
        nc.vector.tensor_copy(xo_sc[:], xo_plane[:].indirect(idx2[:]))
        w2 = deal("w2", w2_raw, w2_plane, [slice(0, 1), slice(1, PACK)])

        def first_stage(bank, t, weight, codes, scales, first):
            cols = slice(t * P, (t + 1) * P)
            nc.tensor.matmul_mx(
                bank[:], lhsT=weight[0][:, cols].bitcast(E5M2), lhsT_scale=weight[1][:, cols],
                rhs=codes, rhs_scale=scales, start=first, stop=not first,
            )

        a_bank = [ps.tile([P, J], F32, name="a_bank" + str(t)) for t in range(PACK)]
        b_bank = [ps.tile([P, J], F32, name="b_bank" + str(t)) for t in range(PACK)]
        xt_operand = (xt_codes[:].bitcast(E4M3), xt_sc[:])
        xo_operand = (xo_codes[:].bitcast(E2M1), xo_sc[:])
        for t in range(PACK):
            first_stage(a_bank[t], t, w, *xt_operand, True)
        first_stage(b_bank[0], 0, w, *xo_operand, True)
        first_stage(a_bank[0], 0, w2, *xo_operand, False)
        first_stage(b_bank[0], 0, w2, *xt_operand, False)
        for t in range(1, PACK):
            first_stage(a_bank[t], t, w2, *xo_operand, False)
            first_stage(b_bank[t], t, w2, *xt_operand, True)
            first_stage(b_bank[t], t, w, *xo_operand, False)

        a_sb = [sb.tile([P, J], F32, name="a_sb" + str(t)) for t in range(PACK)]
        b_sb = [sb.tile([P, J], F32, name="b_sb" + str(t)) for t in range(PACK)]
        pv_read = [[sb.tile([P, HALF], F32, name="pv_read%d_%d" % (t, h)) for h in range(2)] for t in range(PACK)]
        diff = [sb.tile([P, PACK, HALF], F32, name="diff" + str(h)) for h in range(2)]

        def half_of(lst, h):
            return lst[:, h * (HALF // 16) : (h + 1) * (HALF // 16)]

        def empty_a(t):
            nc.vector.tensor_copy(a_sb[t][:], a_bank[t][:])

        def empty_b(t):
            nc.scalar.activation(b_sb[t][:], b_bank[t][:], ACT.Copy)

        def put_a(t):
            nc.vector.tensor_copy(pw[t][:].indirect(idx3[:]), a_sb[t][:])

        def put_b(t):
            nc.scalar.activation(pv[t][:].indirect(idx4[:]), b_sb[t][:], ACT.Copy)

        def read_pv(t, h):
            if (t, h) == (0, 0):
                nc.vector.tensor_copy(pv_read[t][h][:], pv[t][:].indirect(half_of(idx6, h)))
            else:
                nc.scalar.activation(pv_read[t][h][:], pv[t][:].indirect(half_of(idx6, h)), ACT.Copy)

        def read_diff(t, h):
            nc.vector.tensor_tensor(
                diff[h][:, t, :], pw[t][:].indirect(half_of(idx5, h)), pv_read[t][h][:], ALU.subtract
            )

        empty_a(0)
        empty_b(0)
        for t in range(PACK):
            if t + 1 < PACK:
                empty_a(t + 1)
                empty_b(t + 1)
            put_a(t)
            put_b(t)
            if t >= 1:
                read_pv(t - 1, 0)
                if t - 1 < 2:
                    read_pv(t - 1, 1)
        read_pv(3, 0)
        read_pv(2, 1)
        read_pv(3, 1)
        for t, h in ((0, 0), (1, 0), (0, 1), (2, 0), (3, 0), (1, 1), (2, 1), (3, 1)):
            read_diff(t, h)

        for h in range(2):
            hid = sb.tile([P, HALF, PACK], BF16, name="hid" + str(h), align_bytes=64)
            nc.scalar.activation(
                hid[:].rearrange("p (c i) t -> p c t i", i=4),
                diff[h][:].rearrange("p t (c i) -> p c t i", i=4),
                ACT.Abs,
            )
            hid_codes = sb.tile([P, HALF], U32, name="hid_codes" + str(h), align_bytes=64)
            hid_sc = sb.tile([P, HALF], U8, name="hid_sc" + str(h), align_bytes=64)
            nc.vector.quantize_mx(hid_codes[:].bitcast(E4M3), hid_sc[:], hid[:].rearrange("p o t -> p (o t)"))
            for nb in range(2):
                cols = slice(nb * P, (nb + 1) * P)
                y_bank = ps.tile([P, HALF], F32, name=("a_bank", "b_bank")[nb] + str(h))
                nc.tensor.matmul_mx(
                    y_bank[:], lhsT=wb_codes[:, cols].bitcast(E5M2), lhsT_scale=wb_plane[:, cols],
                    rhs=hid_codes[:].bitcast(E4M3), rhs_scale=hid_sc[:], start=True, stop=True,
                )
                y_sb = sb.tile([P, HALF], F32, name="y_sb%d_%d" % (h, nb))
                place = out[cols, h * HALF : (h + 1) * HALF]
                if (h, nb) == (1, 1):
                    nc.scalar.copy(y_sb[:], y_bank[:])
                    nc.scalar.dma_start(place, y_sb[:])
                else:
                    nc.vector.tensor_copy(y_sb[:], y_bank[:])
                    nc.sync.dma_start(place, y_sb[:])
